import numpy as np
import ml_dtypes


def mxq(x, axis, fmt="e4m3"):
    dtype, down = {"e4m3": (ml_dtypes.float8_e4m3fn, 7), "e5m2": (ml_dtypes.float8_e5m2, 14)}[fmt]
    v = np.moveaxis(np.asarray(x, np.float32).astype(ml_dtypes.bfloat16).astype(np.float64), axis, -1)
    blocks = v.reshape(v.shape[:-1] + (-1, 32))
    amax = np.abs(blocks).max(-1, keepdims=True)
    byte = np.maximum(np.where(amax > 0, np.frexp(amax)[1] - 1 + 127, 0) - down, 1)
    scale = np.exp2(byte - 127.0)
    codes = (blocks / scale).astype(np.float32).astype(dtype).astype(np.float64)
    return np.moveaxis((codes * scale).reshape(v.shape), -1, axis)


WIDE = False


def mx_kscale(k):
    if not WIDE:
        return np.ones(k)
    levels = np.array([10, -10, 5, -5, 0])
    if k % 512:
        return np.exp2(np.random.permutation(np.resize(levels, k // 32))).repeat(32)
    a = np.empty((k // 512, 16))
    for p in range(k // 512):
        a[p, :8] = np.random.permutation(np.resize(levels, 8))
        for g in range(8):
            far = levels[np.abs(levels - a[p, g]) >= 10]
            a[p, g + 8] = far[np.random.randint(len(far))]
    return np.exp2(a.ravel()).repeat(32)


def f64(x):
    return np.asarray(x).astype(np.float64)


def striped(idx):
    return np.tile(np.asarray(idx).reshape(-1, 16).T, (8, 1)).astype(np.uint16)


def unstriped(offs):
    return offs[:16].T.reshape(-1).astype(np.int64)


def striped8(idx):
    return np.asarray(idx).reshape(8, -1, 16).transpose(0, 2, 1).reshape(128, -1).astype(np.uint16)


def unstriped8(offs):
    return offs.reshape(8, 16, -1).transpose(0, 2, 1).reshape(8, -1).astype(np.int64)


def pick8(x, idx, run):
    r = np.arange(len(x))
    return x[r[:, None], idx[r % (8 * run) // run]]


E2M1 = np.array([0.0, 0.5, 1.0, 1.5, 2.0, 3.0, 4.0, 6.0, -0.0, -0.5, -1.0, -1.5, -2.0, -3.0, -4.0, -6.0])


def pack_weight(w, fmt):
    k, n = w.shape
    w = f64(np.asarray(w, np.float32).astype(ml_dtypes.bfloat16)).reshape(k // 32, 32, n)
    amax = np.abs(w).max(1)
    if fmt == "e4m3":
        byte = np.frexp(amax)[1] - 1 + 127 - 7
    else:
        mant, ex = np.frexp(amax / 6.0)
        byte = np.where(mant > 0.5, ex, ex - 1) + 127
    byte = np.clip(np.where(amax > 0, byte, 1), 1, 254)
    scaled = (w * np.exp2(127.0 - byte)[:, None, :]).reshape(k, n).astype(np.float32)
    by_word = np.ascontiguousarray(scaled.reshape(k // 512, 128, 4, n).transpose(0, 1, 3, 2))
    if fmt == "e4m3":
        words = by_word.astype(ml_dtypes.float8_e4m3fn).view(np.uint8)
    else:
        c = by_word.astype(ml_dtypes.float4_e2m1fn).view(np.uint8) & 0xF
        words = (c[..., 0::2] | (c[..., 1::2] << 4)).reshape(k // 512, 128, 2 * n)
    return np.ascontiguousarray(words), np.ascontiguousarray(byte.astype(np.uint8).reshape(k // 512, 16, n))


def unpack_weight(words, scales, fmt):
    g, _, n = scales.shape
    words = np.ascontiguousarray(words).reshape(g, 128, n, -1)
    if fmt == "e4m3":
        vals = words.view(ml_dtypes.float8_e4m3fn).astype(np.float64)
    else:
        nib = np.empty((g, 128, n, 4), np.uint8)
        nib[..., 0::2] = words & 0xF
        nib[..., 1::2] = words >> 4
        vals = E2M1[nib]
    vals = vals * np.repeat(np.exp2(scales.astype(np.float64) - 127.0), 8, axis=1)[..., None]
    return vals.transpose(0, 1, 3, 2).reshape(g * 512, n)


K, J, R, T, U, Z, M, O, C, N, S = 512, 256, 512, 512, 512, 512, 1024, 128, 512, 256, 512


def setup_inputs():
    n = np.random.standard_normal
    idx = np.stack([np.random.permutation(T)[:J] for _ in range(8)])
    idx2 = np.stack([np.random.permutation(U)[:J] for _ in range(8)])
    idx3 = np.random.permutation(M)[:J]
    idx4 = np.stack([np.random.permutation(C)[:J] for _ in range(8)])
    idx5 = np.stack([np.random.permutation(C)[:O] for _ in range(8)])
    idx6 = np.stack([np.random.permutation(J)[:O] for _ in range(8)])
    idx7 = np.stack([np.random.permutation(S)[:N] for _ in range(8)])
    fk = mx_kscale(K)
    fr = mx_kscale(R)
    fz = mx_kscale(Z)
    wp = pack_weight(n((K, R)) * 1 / np.sqrt(K) / fk[:, None] * fr, "e2m1")
    xop = pack_weight(n((Z, M)) / fz[:, None], "e2m1")
    w2p = pack_weight(n((Z, R)) * 1 / np.sqrt(Z) * fz[:, None] * fr, "e4m3")
    return {
        "ta": (np.random.randint(-7, 8, (K, T)).astype(np.float64)).astype(np.float32),
        "tb": (np.random.randint(-7, 8, (K, U)).astype(np.float64)).astype(np.float32),
        "ga": ((np.random.randint(10, 25, (K, 1)) / 64.0) * fk[:, None]).astype(np.float32),
        "gb": ((np.random.randint(4, 13, (K, 1)) / 64.0) * fk[:, None]).astype(np.float32),
        "w_words": wp[0],
        "w_scales": wp[1],
        "xo_words": xop[0],
        "xo_scales": xop[1],
        "w2_words": w2p[0],
        "w2_scales": w2p[1],
        "sa": (np.random.uniform(0.5, 1.6, (R, 1))).astype(np.float32),
        "sb": (np.random.uniform(0.5, 1.6, (R, 1))).astype(np.float32),
        "va": (np.random.randint(-7, 8, (R, S)).astype(np.float64)).astype(np.float32),
        "ea": ((np.random.randint(8, 25, (R, 1)) / 1024.0) / fr[:, None]).astype(np.float32),
        "offs": striped8(idx),
        "offs2": striped8(idx2),
        "offs3": striped(idx3),
        "offs4": striped8(idx4),
        "offs5": striped8(idx5),
        "offs6": striped8(idx6),
        "offs7": striped8(idx7),
    }


def reference(ta, tb, ga, gb, w_words, w_scales, xo_words, xo_scales, w2_words, w2_scales, sa, sb, va, ea, offs, offs2, offs3, offs4, offs5, offs6, offs7):
    idx = unstriped8(offs)
    idx2 = unstriped8(offs2)
    idx3 = unstriped(offs3)
    idx4 = unstriped8(offs4)
    idx5 = unstriped8(offs5)
    idx6 = unstriped8(offs6)
    idx7 = unstriped8(offs7)
    wu = unpack_weight(w_words, w_scales, "e2m1")
    xou = unpack_weight(xo_words, xo_scales, "e2m1")
    w2u = unpack_weight(w2_words, w2_scales, "e4m3")
    xc = pick8(f64(ta), idx, 64) * f64(ga) + pick8(f64(tb), idx2, 64) * f64(gb)
    xcq = mxq(xc, 0, "e4m3")
    a = wu.T @ xcq
    xoidx3g = xou[:, idx3]
    b = w2u.T @ xoidx3g
    pw = np.zeros((R, C))
    pw[np.arange(R)[:, None], idx4[np.arange(R) % 512 // 64]] = a
    hid = np.maximum(pick8(pw, idx5, 64) * f64(sa), pick8(b, idx6, 64) * f64(sb))
    vc = pick8(f64(va), idx7, 64) * f64(ea)
    vcq = mxq(vc, 0, "e4m3")
    hidq = mxq(hid, 0, "e4m3")
    y = vcq.T @ hidq
    return y

@@ -1,0 +1,230 @@
+from contextlib import ExitStack
+
+import concourse.mybir as mybir
+
+F32 = mybir.dt.float32
+BF16 = mybir.dt.bfloat16
+I32 = mybir.dt.int32
+U32 = mybir.dt.uint32
+U16 = mybir.dt.uint16
+U8 = mybir.dt.uint8
+FP8X4 = mybir.dt.float8_e4m3fn_x4
+FP4X4 = mybir.dt.float4_e2m1fn_x4
+COPY = mybir.ActivationFunctionType.Copy
+ADD = mybir.AluOpType.add
+MAX = mybir.AluOpType.max
+
+P = 128
+PACK = 4
+QUADS = 4
+SLOTS = 256
+PLACES = 128
+BOARD = 512
+HIDDEN = 512
+NOTES = 1024
+OUTS = 256
+FLOPS = 2 * 512 * 512 * 256 * 2 + 2 * 512 * 256 * 128
+
+
+def tile_picked_twobooks_plain_two_boardmeet_codes_plain_kernel(
+    tc, ta, tb, ga, gb, w_words, w_scales, xo_words, xo_scales, w2_words, w2_scales,
+    sa, sb, va, ea, offs, offs2, offs3, offs4, offs5, offs6, offs7, out,
+):
+    nc = tc.nc
+    with ExitStack() as ctx:
+        lists = ctx.enter_context(tc.tile_pool(name="lists", bufs=1))
+        sbuf = ctx.enter_context(tc.tile_pool(name="sbuf", bufs=1))
+        psum = ctx.enter_context(tc.psum_pool(name="psum", bufs=1))
+
+        def load_list(src, name):
+            t = lists.tile(list(src.shape), U16, name=name)
+            nc.sync.dma_start(t[:], src)
+            return t
+
+        def load_column(src, name):
+            t = sbuf.tile([P, PACK], F32, name=name)
+            nc.sync.dma_start(t[:], src.rearrange("(p t) o -> p (t o)", t=PACK))
+            return t
+
+        def load_rows(src, t, name):
+            rows = sbuf.tile([P, src.shape[1]], F32, name=name, tag=name)
+            nc.sync.dma_start(rows[:], src.rearrange("(p t) c -> p t c", t=PACK)[:, t, :])
+            return rows
+
+        def load_scales(src, name):
+            width = src.shape[2]
+            stage = sbuf.tile([PACK, QUADS, width // 4], I32, name=name + "_stage")
+            nc.sync.dma_start(stage[:], src[0].bitcast(I32).rearrange("(q i) n -> i q n", i=PACK))
+            plane = sbuf.tile([P, width], U8, name=name + "_plane")
+            nc.vector.memset(plane[:].bitcast(I32), 0)
+            for q in range(QUADS):
+                nc.vector.tensor_copy(plane[32 * q : 32 * q + PACK, :].bitcast(I32), stage[:, q, :])
+            return plane
+
+        def deal_scales(plane, name):
+            dealt = sbuf.tile([P, HIDDEN], U8, name=name, align_bytes=64)
+            nc.vector.tensor_copy(
+                dealt[:].rearrange("p (t m) -> p t m", t=PACK),
+                plane[:].rearrange("p (m t) -> p t m", t=PACK),
+            )
+            return dealt
+
+        def fetch(dst, window, offsets, column, t):
+            nc.scalar.activation(dst, window[:].indirect(offsets), COPY, scale=column[:, t : t + 1])
+
+        boards = [sbuf.tile([P, BOARD], F32, name="board%d" % t) for t in range(PACK)]
+        for t in range(PACK):
+            nc.vector.memset(boards[t][:], 0.0)
+
+        w_raw = sbuf.tile([P, HIDDEN], U16, name="w_raw")
+        nc.sync.dma_start(w_raw[:].bitcast(I32), w_words[0].bitcast(I32))
+        l1 = load_list(offs, "l1")
+        ga_t = load_column(ga, "ga_t")
+        ta_t = [load_rows(ta, 0, "ta0")]
+        l2 = load_list(offs2, "l2")
+        gb_t = load_column(gb, "gb_t")
+        tb_t = [load_rows(tb, 0, "tb0")]
+        w_plane = load_scales(w_scales, "w")
+        ta_t.append(load_rows(ta, 1, "ta1"))
+        xo_plane = load_scales(xo_scales, "xo")
+        tb_t.append(load_rows(tb, 1, "tb1"))
+        l3 = load_list(offs3, "l3")
+        ta_t.append(load_rows(ta, 2, "ta2"))
+        w2_plane = load_scales(w2_scales, "w2")
+        tb_t.append(load_rows(tb, 2, "tb2"))
+        l7 = load_list(offs7, "l7")
+        ta_t.append(load_rows(ta, 3, "ta3"))
+        ea_t = load_column(ea, "ea_t")
+        tb_t.append(load_rows(tb, 3, "tb3"))
+        va_t = [load_rows(va, 0, "va0")]
+        l4 = load_list(offs4, "l4")
+        va_t.append(load_rows(va, 1, "va1"))
+        xo_raw = sbuf.tile([P, NOTES], U16, name="xo_raw", tag="xo_raw")
+        nc.sync.dma_start(xo_raw[:].bitcast(I32), xo_words[0].bitcast(I32))
+        w2_raw = sbuf.tile([P, HIDDEN], U32, name="w2_raw", tag="w2_raw")
+        nc.sync.dma_start(w2_raw[:].bitcast(I32), w2_words[0].rearrange("p n t -> p (n t)").bitcast(I32))
+        l6 = load_list(offs6, "l6")
+        va_t.append(load_rows(va, 2, "va2"))
+        sb_t = load_column(sb, "sb_t")
+        va_t.append(load_rows(va, 3, "va3"))
+        l5 = load_list(offs5, "l5")
+        sa_t = load_column(sa, "sa_t")
+
+        w_codes = sbuf.tile([P, HIDDEN], U16, name="w_codes", align_bytes=64)
+        nc.scalar.copy(
+            w_codes[:].rearrange("p (t m) -> p t m", t=PACK),
+            w_raw[:].rearrange("p (m t) -> p t m", t=PACK),
+        )
+        w_bytes = deal_scales(w_plane, "w_bytes")
+        w2_bytes = deal_scales(w2_plane, "w2_bytes")
+
+        xo_bytes = sbuf.tile([P, SLOTS], U8, name="xo_bytes", align_bytes=64)
+        nc.vector.tensor_copy(xo_bytes[:], xo_plane[:].indirect(l3[:]))
+
+        xa = sbuf.tile([P, PACK, SLOTS], F32, name="xa", tag="xa", align_bytes=64)
+        xb = sbuf.tile([P, PACK, SLOTS], F32, name="xb", tag="xb", align_bytes=64)
+        xc = sbuf.tile([P, SLOTS, PACK], BF16, name="xc", align_bytes=64)
+        half = SLOTS // 2
+
+        def add_pair(t, cols):
+            nc.vector.tensor_tensor(
+                xc[:, cols, t : t + 2],
+                xa[:, t : t + 2, cols].rearrange("p t j -> p j t"),
+                xb[:, t : t + 2, cols].rearrange("p t j -> p j t"),
+                ADD,
+            )
+
+        for t in range(PACK):
+            fetch(xa[:, t, :], ta_t[t], l1[:], ga_t, t)
+            if t < PACK - 1:
+                fetch(xb[:, t, :], tb_t[t], l2[:], gb_t, t)
+            if t == 1:
+                add_pair(0, slice(0, SLOTS))
+        for u in range(2):
+            cols = slice(half * u, half * (u + 1))
+            fetch(xb[:, 3, cols], tb_t[3], l2[:, 8 * u : 8 * (u + 1)], gb_t, 3)
+            add_pair(2, cols)
+        xc_codes = sbuf.tile([P, SLOTS], U32, name="xc_codes", align_bytes=64)
+        xc_bytes = sbuf.tile([P, SLOTS], U8, name="xc_bytes", align_bytes=64)
+        for u in range(2):
+            cols = slice(half * u, half * (u + 1))
+            nc.vector.quantize_mx(
+                xc_codes[:, cols].bitcast(FP8X4), xc_bytes[:, cols], xc[:, cols, :].rearrange("p j t -> p (j t)")
+            )
+        xo_codes = sbuf.tile([P, SLOTS], U16, name="xo_codes", tag="xb", align_bytes=64)
+        nc.vector.tensor_copy(xo_codes[:], xo_raw[:].indirect(l3[:]))
+        w2_codes = sbuf.tile([P, HIDDEN], U32, name="w2_codes", tag="xa", align_bytes=64)
+        nc.vector.tensor_copy(
+            w2_codes[:].rearrange("p (t m) -> p t m", t=PACK),
+            w2_raw[:].rearrange("p (m t) -> p t m", t=PACK),
+        )
+
+
+        a_sb = []
+        for t in range(PACK):
+            cols = slice(P * t, P * (t + 1))
+            acc = psum.tile([P, SLOTS], F32, name="a_acc%d" % t, tag="bank%d" % t)
+            nc.tensor.matmul_mx(
+                acc[:], lhsT=w_codes[:, cols].bitcast(FP4X4), lhsT_scale=w_bytes[:, cols],
+                rhs=xc_codes[:].bitcast(FP8X4), rhs_scale=xc_bytes[:], start=True, stop=True,
+            )
+            a_t = sbuf.tile([P, SLOTS], F32, name="a%d" % t, tag=("xo_raw", "w2_raw", "a2", "a3")[t])
+            nc.scalar.copy(a_t[:], acc[:])
+            a_sb.append(a_t)
+
+        for t in range(PACK):
+            nc.vector.tensor_copy(boards[t][:].indirect(l4[:]), a_sb[t][:])
+
+        b_acc = [psum.tile([P, 2, SLOTS], F32, name="b_acc%d" % u, tag="bank%d" % u) for u in range(2)]
+        bg = sbuf.tile([P, PACK, PLACES], F32, name="bg")
+        for t in range(PACK):
+            cols = slice(P * t, P * (t + 1))
+            nc.tensor.matmul_mx(
+                b_acc[t // 2][:, t % 2, :], lhsT=w2_codes[:, cols].bitcast(FP8X4), lhsT_scale=w2_bytes[:, cols],
+                rhs=xo_codes[:].bitcast(FP4X4), rhs_scale=xo_bytes[:], start=True, stop=True,
+            )
+        for t in range(PACK):
+            b_t = sbuf.tile([P, SLOTS], F32, name="b%d" % t)
+            nc.scalar.copy(b_t[:], b_acc[t // 2][:, t % 2, :])
+            fetch(bg[:, t, :], b_t, l6[:], sb_t, t)
+
+        vc_rows = sbuf.tile([P, PACK, OUTS], BF16, name="vc_rows", tag="vc_rows")
+        for t in range(PACK):
+            fetch(vc_rows[:, t, :], va_t[t], l7[:], ea_t, t)
+        vc = sbuf.tile([P, OUTS, PACK], BF16, name="vc", align_bytes=64)
+        nc.scalar.copy(
+            vc[:].rearrange("p (c i) t -> p c t i", i=4),
+            vc_rows[:].rearrange("p t (c i) -> p c t i", i=4),
+        )
+        vc_codes = sbuf.tile([P, OUTS], U32, name="vc_codes", align_bytes=64)
+        vc_bytes = sbuf.tile([P, OUTS], U8, name="vc_bytes", align_bytes=64)
+        nc.vector.quantize_mx(vc_codes[:].bitcast(FP8X4), vc_bytes[:], vc[:].rearrange("p n t -> p (n t)"))
+
+        pg = sbuf.tile([P, PACK, PLACES], F32, name="pg", tag="vc_rows")
+        for t in range(PACK):
+            fetch(pg[:, t, :], boards[t], l5[:], sa_t, t)
+        hid = sbuf.tile([P, PLACES, PACK], BF16, name="hid", align_bytes=64)
+        nc.vector.tensor_tensor(
+            hid[:].rearrange("p (c i) t -> p c t i", i=4),
+            pg[:].rearrange("p t (c i) -> p c t i", i=4),
+            bg[:].rearrange("p t (c i) -> p c t i", i=4),
+            MAX,
+        )
+        hid_codes = sbuf.tile([P, PLACES], U32, name="hid_codes", align_bytes=64)
+        hid_bytes = sbuf.tile([P, PLACES], U8, name="hid_bytes", align_bytes=64)
+        nc.vector.quantize_mx(hid_codes[:].bitcast(FP8X4), hid_bytes[:], hid[:].rearrange("p o t -> p (o t)"))
+
+        for h in range(OUTS // P):
+            cols = slice(P * h, P * (h + 1))
+            y_acc = psum.tile([P, PLACES], F32, name="y_acc%d" % h)
+            nc.tensor.matmul_mx(
+                y_acc[:], lhsT=vc_codes[:, cols].bitcast(FP8X4), lhsT_scale=vc_bytes[:, cols],
+                rhs=hid_codes[:].bitcast(FP8X4), rhs_scale=hid_bytes[:], start=True, stop=True,
+            )
+            y = sbuf.tile([P, PLACES], F32, name="y%d" % h)
+            if h == 0:
+                nc.vector.tensor_copy(y[:], y_acc[:])
+                nc.sync.dma_start(out[cols, :], y[:])
+            else:
+                nc.scalar.copy(y[:], y_acc[:])
+                nc.scalar.dma_start(out[cols, :], y[:])

@@ -64,8 +64,8 @@ def tile_picked_twobooks_plain_two_boardmeet_codes_plain_kernel(
         def deal_scales(plane, name):
             dealt = sbuf.tile([P, HIDDEN], U8, name=name, align_bytes=64)
             nc.vector.tensor_copy(
-                dealt[:].rearrange("p (t m) -> p t m", t=PACK),
-                plane[:].rearrange("p (m t) -> p t m", t=PACK),
+                dealt[:].rearrange("p (t c i) -> p c t i", t=PACK, i=16),
+                plane[:].rearrange("p (c i t) -> p c t i", t=PACK, i=16),
             )
             return dealt
 
@@ -96,13 +96,13 @@ def tile_picked_twobooks_plain_two_boardmeet_codes_plain_kernel(
         ta_t.append(load_rows(ta, 3, "ta3"))
         ea_t = load_column(ea, "ea_t")
         tb_t.append(load_rows(tb, 3, "tb3"))
-        va_t = [load_rows(va, 0, "va0")]
-        l4 = load_list(offs4, "l4")
-        va_t.append(load_rows(va, 1, "va1"))
-        xo_raw = sbuf.tile([P, NOTES], U16, name="xo_raw", tag="xo_raw")
-        nc.sync.dma_start(xo_raw[:].bitcast(I32), xo_words[0].bitcast(I32))
         w2_raw = sbuf.tile([P, HIDDEN], U32, name="w2_raw", tag="w2_raw")
         nc.sync.dma_start(w2_raw[:].bitcast(I32), w2_words[0].rearrange("p n t -> p (n t)").bitcast(I32))
+        va_t = [load_rows(va, 0, "va0")]
+        l4 = load_list(offs4, "l4")
+        xo_raw = sbuf.tile([P, NOTES], U16, name="xo_raw", tag="xo_raw")
+        nc.sync.dma_start(xo_raw[:].bitcast(I32), xo_words[0].bitcast(I32))
+        va_t.append(load_rows(va, 1, "va1"))
         l6 = load_list(offs6, "l6")
         va_t.append(load_rows(va, 2, "va2"))
         sb_t = load_column(sb, "sb_t")
@@ -112,8 +112,8 @@ def tile_picked_twobooks_plain_two_boardmeet_codes_plain_kernel(
 
         w_codes = sbuf.tile([P, HIDDEN], U16, name="w_codes", align_bytes=64)
         nc.scalar.copy(
-            w_codes[:].rearrange("p (t m) -> p t m", t=PACK),
-            w_raw[:].rearrange("p (m t) -> p t m", t=PACK),
+            w_codes[:].rearrange("p (t c i) -> p c t i", t=PACK, i=8),
+            w_raw[:].rearrange("p (c i t) -> p c t i", t=PACK, i=8),
         )
         w_bytes = deal_scales(w_plane, "w_bytes")
         w2_bytes = deal_scales(w2_plane, "w2_bytes")
@@ -126,24 +126,19 @@ def tile_picked_twobooks_plain_two_boardmeet_codes_plain_kernel(
         xc = sbuf.tile([P, SLOTS, PACK], BF16, name="xc", align_bytes=64)
         half = SLOTS // 2
 
-        def add_pair(t, cols):
-            nc.vector.tensor_tensor(
-                xc[:, cols, t : t + 2],
-                xa[:, t : t + 2, cols].rearrange("p t j -> p j t"),
-                xb[:, t : t + 2, cols].rearrange("p t j -> p j t"),
-                ADD,
-            )
-
         for t in range(PACK):
             fetch(xa[:, t, :], ta_t[t], l1[:], ga_t, t)
             if t < PACK - 1:
                 fetch(xb[:, t, :], tb_t[t], l2[:], gb_t, t)
-            if t == 1:
-                add_pair(0, slice(0, SLOTS))
         for u in range(2):
             cols = slice(half * u, half * (u + 1))
             fetch(xb[:, 3, cols], tb_t[3], l2[:, 8 * u : 8 * (u + 1)], gb_t, 3)
-            add_pair(2, cols)
+            nc.vector.tensor_tensor(
+                xc[:, cols, :].rearrange("p (c i) t -> p c t i", i=4),
+                xa[:, :, cols].rearrange("p t (c i) -> p c t i", i=4),
+                xb[:, :, cols].rearrange("p t (c i) -> p c t i", i=4),
+                ADD,
+            )
         xc_codes = sbuf.tile([P, SLOTS], U32, name="xc_codes", align_bytes=64)
         xc_bytes = sbuf.tile([P, SLOTS], U8, name="xc_bytes", align_bytes=64)
         for u in range(2):
@@ -151,16 +146,17 @@ def tile_picked_twobooks_plain_two_boardmeet_codes_plain_kernel(
             nc.vector.quantize_mx(
                 xc_codes[:, cols].bitcast(FP8X4), xc_bytes[:, cols], xc[:, cols, :].rearrange("p j t -> p (j t)")
             )
-        xo_codes = sbuf.tile([P, SLOTS], U16, name="xo_codes", tag="xb", align_bytes=64)
-        nc.vector.tensor_copy(xo_codes[:], xo_raw[:].indirect(l3[:]))
         w2_codes = sbuf.tile([P, HIDDEN], U32, name="w2_codes", tag="xa", align_bytes=64)
         nc.vector.tensor_copy(
-            w2_codes[:].rearrange("p (t m) -> p t m", t=PACK),
-            w2_raw[:].rearrange("p (m t) -> p t m", t=PACK),
+            w2_codes[:].rearrange("p (t c i) -> p c t i", t=PACK, i=4),
+            w2_raw[:].rearrange("p (c i t) -> p c t i", t=PACK, i=4),
         )
+        xo_codes = sbuf.tile([P, SLOTS], U16, name="xo_codes", tag="xb", align_bytes=64)
+        nc.vector.tensor_copy(xo_codes[:], xo_raw[:].indirect(l3[:]))
 
-
-        a_sb = []
+        a_first = sbuf.tile([P, SLOTS], F32, name="a_first", tag="w2_raw")
+        a_rest = sbuf.tile([P, PACK - 1, SLOTS], F32, name="a_rest", tag="xo_raw")
+        a_sb = [a_first[:]] + [a_rest[:, t, :] for t in range(PACK - 1)]
         for t in range(PACK):
             cols = slice(P * t, P * (t + 1))
             acc = psum.tile([P, SLOTS], F32, name="a_acc%d" % t, tag="bank%d" % t)
@@ -168,12 +164,10 @@ def tile_picked_twobooks_plain_two_boardmeet_codes_plain_kernel(
                 acc[:], lhsT=w_codes[:, cols].bitcast(FP4X4), lhsT_scale=w_bytes[:, cols],
                 rhs=xc_codes[:].bitcast(FP8X4), rhs_scale=xc_bytes[:], start=True, stop=True,
             )
-            a_t = sbuf.tile([P, SLOTS], F32, name="a%d" % t, tag=("xo_raw", "w2_raw", "a2", "a3")[t])
-            nc.scalar.copy(a_t[:], acc[:])
-            a_sb.append(a_t)
+            nc.scalar.copy(a_sb[t], acc[:])
 
         for t in range(PACK):
-            nc.vector.tensor_copy(boards[t][:].indirect(l4[:]), a_sb[t][:])
+            nc.vector.tensor_copy(boards[t][:].indirect(l4[:]), a_sb[t])
 
         b_acc = [psum.tile([P, 2, SLOTS], F32, name="b_acc%d" % u, tag="bank%d" % u) for u in range(2)]
         bg = sbuf.tile([P, PACK, PLACES], F32, name="bg")
@@ -191,28 +185,35 @@ def tile_picked_twobooks_plain_two_boardmeet_codes_plain_kernel(
         vc_rows = sbuf.tile([P, PACK, OUTS], BF16, name="vc_rows", tag="vc_rows")
         for t in range(PACK):
             fetch(vc_rows[:, t, :], va_t[t], l7[:], ea_t, t)
-        vc = sbuf.tile([P, OUTS, PACK], BF16, name="vc", align_bytes=64)
-        nc.scalar.copy(
-            vc[:].rearrange("p (c i) t -> p c t i", i=4),
-            vc_rows[:].rearrange("p t (c i) -> p c t i", i=4),
-        )
         vc_codes = sbuf.tile([P, OUTS], U32, name="vc_codes", align_bytes=64)
         vc_bytes = sbuf.tile([P, OUTS], U8, name="vc_bytes", align_bytes=64)
+        vc = sbuf.tile([P, OUTS, PACK], BF16, name="vc", align_bytes=64)
+        for h, move in enumerate((nc.scalar.copy, nc.vector.tensor_copy)):
+            cols = slice(P * h, P * (h + 1))
+            move(
+                vc[:, cols, :].rearrange("p (c i) t -> p c t i", i=4),
+                vc_rows[:, :, cols].rearrange("p t (c i) -> p c t i", i=4),
+            )
         nc.vector.quantize_mx(vc_codes[:].bitcast(FP8X4), vc_bytes[:], vc[:].rearrange("p n t -> p (n t)"))
 
-        pg = sbuf.tile([P, PACK, PLACES], F32, name="pg", tag="vc_rows")
+        pg = sbuf.tile([P, PACK, PLACES], F32, name="pg", tag="va3")
         for t in range(PACK):
             fetch(pg[:, t, :], boards[t], l5[:], sa_t, t)
         hid = sbuf.tile([P, PLACES, PACK], BF16, name="hid", align_bytes=64)
-        nc.vector.tensor_tensor(
-            hid[:].rearrange("p (c i) t -> p c t i", i=4),
-            pg[:].rearrange("p t (c i) -> p c t i", i=4),
-            bg[:].rearrange("p t (c i) -> p c t i", i=4),
-            MAX,
-        )
         hid_codes = sbuf.tile([P, PLACES], U32, name="hid_codes", align_bytes=64)
         hid_bytes = sbuf.tile([P, PLACES], U8, name="hid_bytes", align_bytes=64)
-        nc.vector.quantize_mx(hid_codes[:].bitcast(FP8X4), hid_bytes[:], hid[:].rearrange("p o t -> p (o t)"))
+        halves = [slice(0, PLACES // 2), slice(PLACES // 2, PLACES)]
+        for cols in halves:
+            nc.vector.tensor_tensor(
+                hid[:, cols, :].rearrange("p (c i) t -> p c t i", i=4),
+                pg[:, :, cols].rearrange("p t (c i) -> p c t i", i=4),
+                bg[:, :, cols].rearrange("p t (c i) -> p c t i", i=4),
+                MAX,
+            )
+        for cols in halves:
+            nc.vector.quantize_mx(
+                hid_codes[:, cols].bitcast(FP8X4), hid_bytes[:, cols], hid[:, cols, :].rearrange("p o t -> p (o t)")
+            )
 
         for h in range(OUTS // P):
             cols = slice(P * h, P * (h + 1))

@@ -51,27 +51,13 @@ def tile_picked_twobooks_plain_two_boardmeet_codes_plain_kernel(
             nc.sync.dma_start(rows[:], src.rearrange("(p t) c -> p t c", t=PACK)[:, t, :])
             return rows
 
-        def load_scales(src, name):
-            width = src.shape[2]
-            stage = sbuf.tile([PACK, QUADS, width // 4], I32, name=name + "_stage")
-            nc.sync.dma_start(stage[:], src[0].bitcast(I32).rearrange("(q i) n -> i q n", i=PACK))
-            plane = sbuf.tile([P, width], U8, name=name + "_plane")
-            nc.vector.memset(plane[:].bitcast(I32), 0)
-            for q in range(QUADS):
-                nc.vector.tensor_copy(plane[32 * q : 32 * q + PACK, :].bitcast(I32), stage[:, q, :])
-            return plane
-
-        def deal_scales(plane, name):
-            dealt = sbuf.tile([P, HIDDEN], U8, name=name, align_bytes=64)
-            nc.vector.tensor_copy(
-                dealt[:].rearrange("p (t c i) -> p c t i", t=PACK, i=16),
-                plane[:].rearrange("p (c i t) -> p c t i", t=PACK, i=16),
-            )
-            return dealt
-
         def fetch(dst, window, offsets, column, t):
             nc.scalar.activation(dst, window[:].indirect(offsets), COPY, scale=column[:, t : t + 1])
 
+        xo_stage = sbuf.tile([P, 2, NOTES // 4], I32, name="xo_stage")
+        nc.vector.memset(xo_stage[64:128], 0)
+        ww_plane = sbuf.tile([P, 2, HIDDEN], U8, name="ww_plane")
+        nc.vector.memset(ww_plane[:].rearrange("p s n -> p (s n)").bitcast(I32), 0)
         boards = [sbuf.tile([P, BOARD], F32, name="board%d" % t) for t in range(PACK)]
         for t in range(PACK):
             nc.vector.memset(boards[t][:], 0.0)
@@ -84,24 +70,40 @@ def tile_picked_twobooks_plain_two_boardmeet_codes_plain_kernel(
         l2 = load_list(offs2, "l2")
         gb_t = load_column(gb, "gb_t")
         tb_t = [load_rows(tb, 0, "tb0")]
-        w_plane = load_scales(w_scales, "w")
+        ww_stage = sbuf.tile([PACK, QUADS, 2, HIDDEN // 4], I32, name="ww_stage")
+        for s, src in enumerate((w_scales, w2_scales)):
+            nc.sync.dma_start(ww_stage[:, :, s, :], src[0].bitcast(I32).rearrange("(q i) n -> i q n", i=PACK))
+        for q in range(QUADS):
+            nc.vector.tensor_copy(
+                ww_plane[32 * q : 32 * q + PACK].rearrange("p s n -> p (s n)").bitcast(I32),
+                ww_stage[:, q].rearrange("p s n -> p (s n)"),
+            )
+        ww_bytes = sbuf.tile([P, 2, HIDDEN], U8, name="ww_bytes", align_bytes=64)
+        nc.vector.tensor_copy(
+            ww_bytes[:].rearrange("p s (t c i) -> p s c t i", t=PACK, i=16),
+            ww_plane[:].rearrange("p s (c i t) -> p s c t i", t=PACK, i=16),
+        )
+        w_bytes, w2_bytes = ww_bytes[:, 0, :], ww_bytes[:, 1, :]
         ta_t.append(load_rows(ta, 1, "ta1"))
-        xo_plane = load_scales(xo_scales, "xo")
+        xo_rows = xo_scales[0].bitcast(I32).rearrange("(b h i) n -> h i b n", b=2, h=2)
+        for h in range(2):
+            nc.sync.dma_start(xo_stage[64 + 32 * h : 64 + 32 * h + PACK], xo_rows[h])
+        xo_plane = sbuf.tile([P, NOTES], U8, name="xo_plane")
+        for b in range(2):
+            nc.vector.tensor_copy(xo_plane[64 * b : 64 * (b + 1), :].bitcast(I32), xo_stage[64:128, b, :])
         tb_t.append(load_rows(tb, 1, "tb1"))
         l3 = load_list(offs3, "l3")
-        ta_t.append(load_rows(ta, 2, "ta2"))
-        w2_plane = load_scales(w2_scales, "w2")
-        tb_t.append(load_rows(tb, 2, "tb2"))
-        l7 = load_list(offs7, "l7")
-        ta_t.append(load_rows(ta, 3, "ta3"))
-        ea_t = load_column(ea, "ea_t")
-        tb_t.append(load_rows(tb, 3, "tb3"))
+        for t in range(2, PACK):
+            ta_t.append(load_rows(ta, t, "ta%d" % t))
+            tb_t.append(load_rows(tb, t, "tb%d" % t))
         w2_raw = sbuf.tile([P, HIDDEN], U32, name="w2_raw", tag="w2_raw")
         nc.sync.dma_start(w2_raw[:].bitcast(I32), w2_words[0].rearrange("p n t -> p (n t)").bitcast(I32))
+        l7 = load_list(offs7, "l7")
+        ea_t = load_column(ea, "ea_t")
         va_t = [load_rows(va, 0, "va0")]
-        l4 = load_list(offs4, "l4")
         xo_raw = sbuf.tile([P, NOTES], U16, name="xo_raw", tag="xo_raw")
         nc.sync.dma_start(xo_raw[:].bitcast(I32), xo_words[0].bitcast(I32))
+        l4 = load_list(offs4, "l4")
         va_t.append(load_rows(va, 1, "va1"))
         l6 = load_list(offs6, "l6")
         va_t.append(load_rows(va, 2, "va2"))
@@ -115,8 +117,6 @@ def tile_picked_twobooks_plain_two_boardmeet_codes_plain_kernel(
             w_codes[:].rearrange("p (t c i) -> p c t i", t=PACK, i=8),
             w_raw[:].rearrange("p (c i t) -> p c t i", t=PACK, i=8),
         )
-        w_bytes = deal_scales(w_plane, "w_bytes")
-        w2_bytes = deal_scales(w2_plane, "w2_bytes")
 
         xo_bytes = sbuf.tile([P, SLOTS], U8, name="xo_bytes", align_bytes=64)
         nc.vector.tensor_copy(xo_bytes[:], xo_plane[:].indirect(l3[:]))
@@ -126,19 +126,24 @@ def tile_picked_twobooks_plain_two_boardmeet_codes_plain_kernel(
         xc = sbuf.tile([P, SLOTS, PACK], BF16, name="xc", align_bytes=64)
         half = SLOTS // 2
 
+        def add_pair(t, cols):
+            nc.vector.tensor_tensor(
+                xc[:, cols, t : t + 2],
+                xa[:, t : t + 2, cols].rearrange("p t j -> p j t"),
+                xb[:, t : t + 2, cols].rearrange("p t j -> p j t"),
+                ADD,
+            )
+
         for t in range(PACK):
             fetch(xa[:, t, :], ta_t[t], l1[:], ga_t, t)
             if t < PACK - 1:
                 fetch(xb[:, t, :], tb_t[t], l2[:], gb_t, t)
+            if t == 1:
+                add_pair(0, slice(0, SLOTS))
         for u in range(2):
             cols = slice(half * u, half * (u + 1))
             fetch(xb[:, 3, cols], tb_t[3], l2[:, 8 * u : 8 * (u + 1)], gb_t, 3)
-            nc.vector.tensor_tensor(
-                xc[:, cols, :].rearrange("p (c i) t -> p c t i", i=4),
-                xa[:, :, cols].rearrange("p t (c i) -> p c t i", i=4),
-                xb[:, :, cols].rearrange("p t (c i) -> p c t i", i=4),
-                ADD,
-            )
+            add_pair(2, cols)
         xc_codes = sbuf.tile([P, SLOTS], U32, name="xc_codes", align_bytes=64)
         xc_bytes = sbuf.tile([P, SLOTS], U8, name="xc_bytes", align_bytes=64)
         for u in range(2):
@@ -157,19 +162,20 @@ def tile_picked_twobooks_plain_two_boardmeet_codes_plain_kernel(
         a_first = sbuf.tile([P, SLOTS], F32, name="a_first", tag="w2_raw")
         a_rest = sbuf.tile([P, PACK - 1, SLOTS], F32, name="a_rest", tag="xo_raw")
         a_sb = [a_first[:]] + [a_rest[:, t, :] for t in range(PACK - 1)]
-        for t in range(PACK):
+        pieces = [(0, 0, half), (0, half, SLOTS)] + [(t, 0, SLOTS) for t in range(1, PACK)]
+        for n, (t, j0, j1) in enumerate(pieces):
             cols = slice(P * t, P * (t + 1))
-            acc = psum.tile([P, SLOTS], F32, name="a_acc%d" % t, tag="bank%d" % t)
+            acc = psum.tile([P, j1 - j0], F32, name="a_acc%d" % n, tag="bank%d" % n)
             nc.tensor.matmul_mx(
                 acc[:], lhsT=w_codes[:, cols].bitcast(FP4X4), lhsT_scale=w_bytes[:, cols],
-                rhs=xc_codes[:].bitcast(FP8X4), rhs_scale=xc_bytes[:], start=True, stop=True,
+                rhs=xc_codes[:, j0:j1].bitcast(FP8X4), rhs_scale=xc_bytes[:, j0:j1], start=True, stop=True,
             )
-            nc.scalar.copy(a_sb[t], acc[:])
+            nc.scalar.copy(a_sb[t][:, j0:j1], acc[:])
 
-        for t in range(PACK):
-            nc.vector.tensor_copy(boards[t][:].indirect(l4[:]), a_sb[t])
+        for t, j0, j1 in pieces:
+            nc.vector.tensor_copy(boards[t][:].indirect(l4[:, j0 // 16 : j1 // 16]), a_sb[t][:, j0:j1])
 
-        b_acc = [psum.tile([P, 2, SLOTS], F32, name="b_acc%d" % u, tag="bank%d" % u) for u in range(2)]
+        b_acc = [psum.tile([P, 2, SLOTS], F32, name="b_acc%d" % u, tag="bank%d" % (u + 1)) for u in range(2)]
         bg = sbuf.tile([P, PACK, PLACES], F32, name="bg")
         for t in range(PACK):
             cols = slice(P * t, P * (t + 1))

@@ -12,6 +12,7 @@ FP8X4 = mybir.dt.float8_e4m3fn_x4
 FP4X4 = mybir.dt.float4_e2m1fn_x4
 COPY = mybir.ActivationFunctionType.Copy
 ADD = mybir.AluOpType.add
+MULT = mybir.AluOpType.mult
 MAX = mybir.AluOpType.max
 
 P = 128
@@ -42,7 +43,7 @@ def tile_picked_twobooks_plain_two_boardmeet_codes_plain_kernel(
             return t
 
         def load_column(src, name):
-            t = sbuf.tile([P, PACK], F32, name=name)
+            t = sbuf.tile([P, PACK], F32, name=name, tag=name)
             nc.sync.dma_start(t[:], src.rearrange("(p t) o -> p (t o)", t=PACK))
             return t
 
@@ -98,12 +99,12 @@ def tile_picked_twobooks_plain_two_boardmeet_codes_plain_kernel(
             tb_t.append(load_rows(tb, t, "tb%d" % t))
         w2_raw = sbuf.tile([P, HIDDEN], U32, name="w2_raw", tag="w2_raw")
         nc.sync.dma_start(w2_raw[:].bitcast(I32), w2_words[0].rearrange("p n t -> p (n t)").bitcast(I32))
-        l7 = load_list(offs7, "l7")
-        ea_t = load_column(ea, "ea_t")
-        va_t = [load_rows(va, 0, "va0")]
         xo_raw = sbuf.tile([P, NOTES], U16, name="xo_raw", tag="xo_raw")
         nc.sync.dma_start(xo_raw[:].bitcast(I32), xo_words[0].bitcast(I32))
         l4 = load_list(offs4, "l4")
+        l7 = load_list(offs7, "l7")
+        ea_t = load_column(ea, "ea_t")
+        va_t = [load_rows(va, 0, "va0")]
         va_t.append(load_rows(va, 1, "va1"))
         l6 = load_list(offs6, "l6")
         va_t.append(load_rows(va, 2, "va2"))
@@ -121,7 +122,7 @@ def tile_picked_twobooks_plain_two_boardmeet_codes_plain_kernel(
         xo_bytes = sbuf.tile([P, SLOTS], U8, name="xo_bytes", align_bytes=64)
         nc.vector.tensor_copy(xo_bytes[:], xo_plane[:].indirect(l3[:]))
 
-        xa = sbuf.tile([P, PACK, SLOTS], F32, name="xa", tag="xa", align_bytes=64)
+        xa = sbuf.tile([P, PACK, SLOTS], F32, name="xa")
         xb = sbuf.tile([P, PACK, SLOTS], F32, name="xb", tag="xb", align_bytes=64)
         xc = sbuf.tile([P, SLOTS, PACK], BF16, name="xc", align_bytes=64)
         half = SLOTS // 2
@@ -151,15 +152,15 @@ def tile_picked_twobooks_plain_two_boardmeet_codes_plain_kernel(
             nc.vector.quantize_mx(
                 xc_codes[:, cols].bitcast(FP8X4), xc_bytes[:, cols], xc[:, cols, :].rearrange("p j t -> p (j t)")
             )
-        w2_codes = sbuf.tile([P, HIDDEN], U32, name="w2_codes", tag="xa", align_bytes=64)
-        nc.vector.tensor_copy(
+        w2_codes = sbuf.tile([P, HIDDEN], U32, name="w2_codes", align_bytes=64)
+        nc.scalar.copy(
             w2_codes[:].rearrange("p (t c i) -> p c t i", t=PACK, i=4),
             w2_raw[:].rearrange("p (c i t) -> p c t i", t=PACK, i=4),
         )
         xo_codes = sbuf.tile([P, SLOTS], U16, name="xo_codes", tag="xb", align_bytes=64)
         nc.vector.tensor_copy(xo_codes[:], xo_raw[:].indirect(l3[:]))
 
-        a_first = sbuf.tile([P, SLOTS], F32, name="a_first", tag="w2_raw")
+        a_first = sbuf.tile([P, SLOTS], F32, name="a_first")
         a_rest = sbuf.tile([P, PACK - 1, SLOTS], F32, name="a_rest", tag="xo_raw")
         a_sb = [a_first[:]] + [a_rest[:, t, :] for t in range(PACK - 1)]
         pieces = [(0, 0, half), (0, half, SLOTS)] + [(t, 0, SLOTS) for t in range(1, PACK)]
@@ -175,8 +176,27 @@ def tile_picked_twobooks_plain_two_boardmeet_codes_plain_kernel(
         for t, j0, j1 in pieces:
             nc.vector.tensor_copy(boards[t][:].indirect(l4[:, j0 // 16 : j1 // 16]), a_sb[t][:, j0:j1])
 
+        vc_rows = sbuf.tile([P, PACK, OUTS], BF16, name="vc_rows", tag="vc_rows")
+        for t in range(PACK):
+            fetch(vc_rows[:, t, :], va_t[t], l7[:], ea_t, t)
+        vc_codes = sbuf.tile([P, OUTS], U32, name="vc_codes", align_bytes=64)
+        vc_bytes = sbuf.tile([P, OUTS], U8, name="vc_bytes", align_bytes=64)
+        vc = sbuf.tile([P, OUTS, PACK], BF16, name="vc", align_bytes=64)
+        for h in range(OUTS // P):
+            cols = slice(P * h, P * (h + 1))
+            nc.gpsimd.tensor_scalar(
+                vc[:, cols, :].rearrange("p (c i) t -> p c t i", i=4),
+                vc_rows[:, :, cols].rearrange("p t (c i) -> p c t i", i=4),
+                1.0, 0.0, MULT, ADD,
+            )
+        for h in range(OUTS // P):
+            cols = slice(P * h, P * (h + 1))
+            nc.vector.quantize_mx(
+                vc_codes[:, cols].bitcast(FP8X4), vc_bytes[:, cols], vc[:, cols, :].rearrange("p n t -> p (n t)")
+            )
+
         b_acc = [psum.tile([P, 2, SLOTS], F32, name="b_acc%d" % u, tag="bank%d" % (u + 1)) for u in range(2)]
-        bg = sbuf.tile([P, PACK, PLACES], F32, name="bg")
+        bg = sbuf.tile([P, PACK, PLACES], F32, name="bg", tag="ea_t")
         for t in range(PACK):
             cols = slice(P * t, P * (t + 1))
             nc.tensor.matmul_mx(
@@ -184,23 +204,9 @@ def tile_picked_twobooks_plain_two_boardmeet_codes_plain_kernel(
                 rhs=xo_codes[:].bitcast(FP4X4), rhs_scale=xo_bytes[:], start=True, stop=True,
             )
         for t in range(PACK):
-            b_t = sbuf.tile([P, SLOTS], F32, name="b%d" % t)
+            b_t = sbuf.tile([P, SLOTS], F32, name="b%d" % t, tag="va%d" % (PACK - 1 - t))
             nc.scalar.copy(b_t[:], b_acc[t // 2][:, t % 2, :])
             fetch(bg[:, t, :], b_t, l6[:], sb_t, t)
-
-        vc_rows = sbuf.tile([P, PACK, OUTS], BF16, name="vc_rows", tag="vc_rows")
-        for t in range(PACK):
-            fetch(vc_rows[:, t, :], va_t[t], l7[:], ea_t, t)
-        vc_codes = sbuf.tile([P, OUTS], U32, name="vc_codes", align_bytes=64)
-        vc_bytes = sbuf.tile([P, OUTS], U8, name="vc_bytes", align_bytes=64)
-        vc = sbuf.tile([P, OUTS, PACK], BF16, name="vc", align_bytes=64)
-        for h, move in enumerate((nc.scalar.copy, nc.vector.tensor_copy)):
-            cols = slice(P * h, P * (h + 1))
-            move(
-                vc[:, cols, :].rearrange("p (c i) t -> p c t i", i=4),
-                vc_rows[:, :, cols].rearrange("p t (c i) -> p c t i", i=4),
-            )
-        nc.vector.quantize_mx(vc_codes[:].bitcast(FP8X4), vc_bytes[:], vc[:].rearrange("p n t -> p (n t)"))
 
         pg = sbuf.tile([P, PACK, PLACES], F32, name="pg", tag="va3")
         for t in range(PACK):

@@ -17,14 +17,17 @@ MAX = mybir.AluOpType.max
 
 P = 128
 PACK = 4
-QUADS = 4
+QUAD = 32
+QUADS = P // QUAD
+LIST_ROWS = 16
+LINE = 16
 SLOTS = 256
 PLACES = 128
 BOARD = 512
 HIDDEN = 512
 NOTES = 1024
 OUTS = 256
-FLOPS = 2 * 512 * 512 * 256 * 2 + 2 * 512 * 256 * 128
+FLOPS = 2 * (2 * 512 * HIDDEN * SLOTS) + 2 * HIDDEN * OUTS * PLACES
 
 
 def tile_picked_twobooks_plain_two_boardmeet_codes_plain_kernel(
@@ -38,96 +41,117 @@ def tile_picked_twobooks_plain_two_boardmeet_codes_plain_kernel(
         psum = ctx.enter_context(tc.psum_pool(name="psum", bufs=1))
 
         def load_list(src, name):
-            t = lists.tile(list(src.shape), U16, name=name)
-            nc.sync.dma_start(t[:], src)
-            return t
+            offsets = lists.tile(list(src.shape), U16, name=name)
+            nc.sync.dma_start(offsets[:], src)
+            return offsets
 
-        def load_column(src, name):
-            t = sbuf.tile([P, PACK], F32, name=name, tag=name)
-            nc.sync.dma_start(t[:], src.rearrange("(p t) o -> p (t o)", t=PACK))
-            return t
+        def load_factors(src, name):
+            factors = sbuf.tile([P, PACK], F32, name=name, tag=name)
+            nc.sync.dma_start(factors[:], src.rearrange("(p t) o -> p (t o)", t=PACK))
+            return factors
 
-        def load_rows(src, t, name):
-            rows = sbuf.tile([P, src.shape[1]], F32, name=name, tag=name)
-            nc.sync.dma_start(rows[:], src.rearrange("(p t) c -> p t c", t=PACK)[:, t, :])
-            return rows
+        def load_plane(src, t, name):
+            plane = sbuf.tile([P, src.shape[1]], F32, name=name, tag=name)
+            nc.sync.dma_start(plane[:], src.rearrange("(p t) c -> p t c", t=PACK)[:, t, :])
+            return plane
 
-        def fetch(dst, window, offsets, column, t):
-            nc.scalar.activation(dst, window[:].indirect(offsets), COPY, scale=column[:, t : t + 1])
+        def fetch(dst, window, offsets, factors, t):
+            nc.scalar.activation(dst, window[:].indirect(offsets), COPY, scale=factors[:, t : t + 1])
+
+        def dealt(columns, run):
+            return columns.rearrange("p (t c i) -> p c t i", t=PACK, i=run)
+
+        def undealt(columns, run):
+            return columns.rearrange("p (c i t) -> p c t i", t=PACK, i=run)
+
+        def as_words(values):
+            return values.rearrange("p (c i) t -> p c t i", i=PACK)
+
+        def as_planes(values):
+            return values.rearrange("p t (c i) -> p c t i", i=PACK)
+
+        def quantize(codes, scales, values, cols):
+            nc.vector.quantize_mx(
+                codes[:, cols].bitcast(FP8X4), scales[:, cols], values[:, cols, :].rearrange("p c t -> p (c t)")
+            )
 
         xo_stage = sbuf.tile([P, 2, NOTES // 4], I32, name="xo_stage")
-        nc.vector.memset(xo_stage[64:128], 0)
-        ww_plane = sbuf.tile([P, 2, HIDDEN], U8, name="ww_plane")
-        nc.vector.memset(ww_plane[:].rearrange("p s n -> p (s n)").bitcast(I32), 0)
+        nc.vector.memset(xo_stage[P // 2 : P], 0)
+        ww_spread = sbuf.tile([P, 2, HIDDEN], U8, name="ww_spread")
+        nc.vector.memset(ww_spread[:].rearrange("p s n -> p (s n)").bitcast(I32), 0)
         boards = [sbuf.tile([P, BOARD], F32, name="board%d" % t) for t in range(PACK)]
         for t in range(PACK):
             nc.vector.memset(boards[t][:], 0.0)
 
         w_raw = sbuf.tile([P, HIDDEN], U16, name="w_raw")
         nc.sync.dma_start(w_raw[:].bitcast(I32), w_words[0].bitcast(I32))
-        l1 = load_list(offs, "l1")
-        ga_t = load_column(ga, "ga_t")
-        ta_t = [load_rows(ta, 0, "ta0")]
-        l2 = load_list(offs2, "l2")
-        gb_t = load_column(gb, "gb_t")
-        tb_t = [load_rows(tb, 0, "tb0")]
+        ta_list = load_list(offs, "ta_list")
+        ga_t = load_factors(ga, "ga_t")
+        ta_t = [load_plane(ta, 0, "ta0")]
+        tb_list = load_list(offs2, "tb_list")
+        gb_t = load_factors(gb, "gb_t")
+        tb_t = [load_plane(tb, 0, "tb0")]
+
         ww_stage = sbuf.tile([PACK, QUADS, 2, HIDDEN // 4], I32, name="ww_stage")
         for s, src in enumerate((w_scales, w2_scales)):
             nc.sync.dma_start(ww_stage[:, :, s, :], src[0].bitcast(I32).rearrange("(q i) n -> i q n", i=PACK))
         for q in range(QUADS):
             nc.vector.tensor_copy(
-                ww_plane[32 * q : 32 * q + PACK].rearrange("p s n -> p (s n)").bitcast(I32),
+                ww_spread[QUAD * q : QUAD * q + PACK].rearrange("p s n -> p (s n)").bitcast(I32),
                 ww_stage[:, q].rearrange("p s n -> p (s n)"),
             )
         ww_bytes = sbuf.tile([P, 2, HIDDEN], U8, name="ww_bytes", align_bytes=64)
         nc.vector.tensor_copy(
-            ww_bytes[:].rearrange("p s (t c i) -> p s c t i", t=PACK, i=16),
-            ww_plane[:].rearrange("p s (c i t) -> p s c t i", t=PACK, i=16),
+            ww_bytes[:].rearrange("p s (t c i) -> p s c t i", t=PACK, i=LINE),
+            ww_spread[:].rearrange("p s (c i t) -> p s c t i", t=PACK, i=LINE),
         )
         w_bytes, w2_bytes = ww_bytes[:, 0, :], ww_bytes[:, 1, :]
-        ta_t.append(load_rows(ta, 1, "ta1"))
-        xo_rows = xo_scales[0].bitcast(I32).rearrange("(b h i) n -> h i b n", b=2, h=2)
-        for h in range(2):
-            nc.sync.dma_start(xo_stage[64 + 32 * h : 64 + 32 * h + PACK], xo_rows[h])
-        xo_plane = sbuf.tile([P, NOTES], U8, name="xo_plane")
-        for b in range(2):
-            nc.vector.tensor_copy(xo_plane[64 * b : 64 * (b + 1), :].bitcast(I32), xo_stage[64:128, b, :])
-        tb_t.append(load_rows(tb, 1, "tb1"))
-        l3 = load_list(offs3, "l3")
+        ta_t.append(load_plane(ta, 1, "ta1"))
+
+        xo_rows = xo_scales[0].bitcast(I32).rearrange("(u v i) n -> v i u n", u=2, v=2)
+        for v in range(2):
+            nc.sync.dma_start(xo_stage[P // 2 + QUAD * v : P // 2 + QUAD * v + PACK], xo_rows[v])
+        xo_spread = sbuf.tile([P, NOTES], U8, name="xo_spread")
+        for u in range(2):
+            nc.vector.tensor_copy(
+                xo_spread[P // 2 * u : P // 2 * (u + 1), :].bitcast(I32), xo_stage[P // 2 : P, u, :]
+            )
+        tb_t.append(load_plane(tb, 1, "tb1"))
+        xo_list = load_list(offs3, "xo_list")
         for t in range(2, PACK):
-            ta_t.append(load_rows(ta, t, "ta%d" % t))
-            tb_t.append(load_rows(tb, t, "tb%d" % t))
-        w2_raw = sbuf.tile([P, HIDDEN], U32, name="w2_raw", tag="w2_raw")
-        nc.sync.dma_start(w2_raw[:].bitcast(I32), w2_words[0].rearrange("p n t -> p (n t)").bitcast(I32))
+            ta_t.append(load_plane(ta, t, "ta%d" % t))
+            tb_t.append(load_plane(tb, t, "tb%d" % t))
+
+        va_list = load_list(offs7, "va_list")
+        ea_t = load_factors(ea, "ea_t")
+        va_t = [load_plane(va, 0, "va0")]
         xo_raw = sbuf.tile([P, NOTES], U16, name="xo_raw", tag="xo_raw")
         nc.sync.dma_start(xo_raw[:].bitcast(I32), xo_words[0].bitcast(I32))
-        l4 = load_list(offs4, "l4")
-        l7 = load_list(offs7, "l7")
-        ea_t = load_column(ea, "ea_t")
-        va_t = [load_rows(va, 0, "va0")]
-        va_t.append(load_rows(va, 1, "va1"))
-        l6 = load_list(offs6, "l6")
-        va_t.append(load_rows(va, 2, "va2"))
-        sb_t = load_column(sb, "sb_t")
-        va_t.append(load_rows(va, 3, "va3"))
-        l5 = load_list(offs5, "l5")
-        sa_t = load_column(sa, "sa_t")
+        put_list = load_list(offs4, "put_list")
+        va_t.append(load_plane(va, 1, "va1"))
+        w2_raw = sbuf.tile([P, HIDDEN], U32, name="w2_raw")
+        nc.sync.dma_start(w2_raw[:].bitcast(I32), w2_words[0].rearrange("p n t -> p (n t)").bitcast(I32))
+        va_t.append(load_plane(va, 2, "va2"))
+        va_t.append(load_plane(va, 3, "va3"))
+        b_list = load_list(offs6, "b_list")
+        sb_t = load_factors(sb, "sb_t")
+        pw_list = load_list(offs5, "pw_list")
+        sa_t = load_factors(sa, "sa_t")
 
         w_codes = sbuf.tile([P, HIDDEN], U16, name="w_codes", align_bytes=64)
-        nc.scalar.copy(
-            w_codes[:].rearrange("p (t c i) -> p c t i", t=PACK, i=8),
-            w_raw[:].rearrange("p (c i t) -> p c t i", t=PACK, i=8),
-        )
-
+        nc.scalar.copy(dealt(w_codes[:], LINE // 2), undealt(w_raw[:], LINE // 2))
         xo_bytes = sbuf.tile([P, SLOTS], U8, name="xo_bytes", align_bytes=64)
-        nc.vector.tensor_copy(xo_bytes[:], xo_plane[:].indirect(l3[:]))
+        nc.vector.tensor_copy(xo_bytes[:], xo_spread[:].indirect(xo_list[:]))
 
         xa = sbuf.tile([P, PACK, SLOTS], F32, name="xa")
         xb = sbuf.tile([P, PACK, SLOTS], F32, name="xb", tag="xb", align_bytes=64)
-        xc = sbuf.tile([P, SLOTS, PACK], BF16, name="xc", align_bytes=64)
-        half = SLOTS // 2
+        xc = sbuf.tile([P, SLOTS, PACK], BF16, name="xc", tag="xc", align_bytes=64)
+        slot_halves = [slice(0, SLOTS // 2), slice(SLOTS // 2, SLOTS)]
 
-        def add_pair(t, cols):
+        def entries(offsets, cols):
+            return offsets[:, cols.start // LIST_ROWS : cols.stop // LIST_ROWS]
+
+        def add_two_planes(t, cols):
             nc.vector.tensor_tensor(
                 xc[:, cols, t : t + 2],
                 xa[:, t : t + 2, cols].rearrange("p t j -> p j t"),
@@ -135,109 +159,88 @@ def tile_picked_twobooks_plain_two_boardmeet_codes_plain_kernel(
                 ADD,
             )
 
-        for t in range(PACK):
-            fetch(xa[:, t, :], ta_t[t], l1[:], ga_t, t)
-            if t < PACK - 1:
-                fetch(xb[:, t, :], tb_t[t], l2[:], gb_t, t)
-            if t == 1:
-                add_pair(0, slice(0, SLOTS))
-        for u in range(2):
-            cols = slice(half * u, half * (u + 1))
-            fetch(xb[:, 3, cols], tb_t[3], l2[:, 8 * u : 8 * (u + 1)], gb_t, 3)
-            add_pair(2, cols)
+        for t in range(2):
+            fetch(xa[:, t, :], ta_t[t], ta_list[:], ga_t, t)
+            fetch(xb[:, t, :], tb_t[t], tb_list[:], gb_t, t)
+        add_two_planes(0, slice(0, SLOTS))
+        fetch(xa[:, 2, :], ta_t[2], ta_list[:], ga_t, 2)
+        fetch(xb[:, 2, :], tb_t[2], tb_list[:], gb_t, 2)
+        fetch(xa[:, 3, :], ta_t[3], ta_list[:], ga_t, 3)
+        for cols in slot_halves:
+            fetch(xb[:, 3, cols], tb_t[3], entries(tb_list, cols), gb_t, 3)
+            add_two_planes(2, cols)
         xc_codes = sbuf.tile([P, SLOTS], U32, name="xc_codes", align_bytes=64)
         xc_bytes = sbuf.tile([P, SLOTS], U8, name="xc_bytes", align_bytes=64)
-        for u in range(2):
-            cols = slice(half * u, half * (u + 1))
-            nc.vector.quantize_mx(
-                xc_codes[:, cols].bitcast(FP8X4), xc_bytes[:, cols], xc[:, cols, :].rearrange("p j t -> p (j t)")
-            )
-        w2_codes = sbuf.tile([P, HIDDEN], U32, name="w2_codes", align_bytes=64)
-        nc.scalar.copy(
-            w2_codes[:].rearrange("p (t c i) -> p c t i", t=PACK, i=4),
-            w2_raw[:].rearrange("p (c i t) -> p c t i", t=PACK, i=4),
-        )
+        for cols in slot_halves:
+            quantize(xc_codes, xc_bytes, xc, cols)
+
+        w2_codes = sbuf.tile([P, HIDDEN], U32, name="w2_codes", tag="xc", align_bytes=64)
+        nc.gpsimd.tensor_copy(dealt(w2_codes[:], LINE // 4), undealt(w2_raw[:], LINE // 4))
         xo_codes = sbuf.tile([P, SLOTS], U16, name="xo_codes", tag="xb", align_bytes=64)
-        nc.vector.tensor_copy(xo_codes[:], xo_raw[:].indirect(l3[:]))
+        nc.vector.tensor_copy(xo_codes[:], xo_raw[:].indirect(xo_list[:]))
 
         a_first = sbuf.tile([P, SLOTS], F32, name="a_first")
         a_rest = sbuf.tile([P, PACK - 1, SLOTS], F32, name="a_rest", tag="xo_raw")
-        a_sb = [a_first[:]] + [a_rest[:, t, :] for t in range(PACK - 1)]
-        pieces = [(0, 0, half), (0, half, SLOTS)] + [(t, 0, SLOTS) for t in range(1, PACK)]
-        for n, (t, j0, j1) in enumerate(pieces):
-            cols = slice(P * t, P * (t + 1))
-            acc = psum.tile([P, j1 - j0], F32, name="a_acc%d" % n, tag="bank%d" % n)
+        a_t = [a_first[:]] + [a_rest[:, t, :] for t in range(PACK - 1)]
+        pieces = [(0, cols) for cols in slot_halves] + [(t, slice(0, SLOTS)) for t in range(1, PACK)]
+        for bank, (t, cols) in enumerate(pieces):
+            stationary = slice(P * t, P * (t + 1))
+            a_acc = psum.tile([P, cols.stop - cols.start], F32, name="a_acc%d" % bank, tag="bank%d" % bank)
             nc.tensor.matmul_mx(
-                acc[:], lhsT=w_codes[:, cols].bitcast(FP4X4), lhsT_scale=w_bytes[:, cols],
-                rhs=xc_codes[:, j0:j1].bitcast(FP8X4), rhs_scale=xc_bytes[:, j0:j1], start=True, stop=True,
+                a_acc[:], lhsT=w_codes[:, stationary].bitcast(FP4X4), lhsT_scale=w_bytes[:, stationary],
+                rhs=xc_codes[:, cols].bitcast(FP8X4), rhs_scale=xc_bytes[:, cols], start=True, stop=True,
             )
-            nc.scalar.copy(a_sb[t][:, j0:j1], acc[:])
+            nc.scalar.copy(a_t[t][:, cols], a_acc[:])
+        for t, cols in pieces:
+            nc.vector.tensor_copy(boards[t][:].indirect(entries(put_list, cols)), a_t[t][:, cols])
 
-        for t, j0, j1 in pieces:
-            nc.vector.tensor_copy(boards[t][:].indirect(l4[:, j0 // 16 : j1 // 16]), a_sb[t][:, j0:j1])
-
-        vc_rows = sbuf.tile([P, PACK, OUTS], BF16, name="vc_rows", tag="vc_rows")
+        vc_planes = sbuf.tile([P, PACK, OUTS], BF16, name="vc_planes")
         for t in range(PACK):
-            fetch(vc_rows[:, t, :], va_t[t], l7[:], ea_t, t)
+            fetch(vc_planes[:, t, :], va_t[t], va_list[:], ea_t, t)
         vc_codes = sbuf.tile([P, OUTS], U32, name="vc_codes", align_bytes=64)
         vc_bytes = sbuf.tile([P, OUTS], U8, name="vc_bytes", align_bytes=64)
-        vc = sbuf.tile([P, OUTS, PACK], BF16, name="vc", align_bytes=64)
-        for h in range(OUTS // P):
-            cols = slice(P * h, P * (h + 1))
-            nc.gpsimd.tensor_scalar(
-                vc[:, cols, :].rearrange("p (c i) t -> p c t i", i=4),
-                vc_rows[:, :, cols].rearrange("p t (c i) -> p c t i", i=4),
-                1.0, 0.0, MULT, ADD,
-            )
-        for h in range(OUTS // P):
-            cols = slice(P * h, P * (h + 1))
-            nc.vector.quantize_mx(
-                vc_codes[:, cols].bitcast(FP8X4), vc_bytes[:, cols], vc[:, cols, :].rearrange("p n t -> p (n t)")
-            )
+        vc = sbuf.tile([P, OUTS, PACK], BF16, name="vc", tag="vc", align_bytes=64)
+        out_halves = [slice(0, P), slice(P, OUTS)]
+        for cols in out_halves:
+            nc.gpsimd.tensor_scalar(as_words(vc[:, cols, :]), as_planes(vc_planes[:, :, cols]), 1.0, 0.0, MULT, ADD)
+        for cols in out_halves:
+            quantize(vc_codes, vc_bytes, vc, cols)
 
         b_acc = [psum.tile([P, 2, SLOTS], F32, name="b_acc%d" % u, tag="bank%d" % (u + 1)) for u in range(2)]
-        bg = sbuf.tile([P, PACK, PLACES], F32, name="bg", tag="ea_t")
+        b_got = sbuf.tile([P, PACK, PLACES], F32, name="b_got", tag="ea_t")
         for t in range(PACK):
-            cols = slice(P * t, P * (t + 1))
+            stationary = slice(P * t, P * (t + 1))
             nc.tensor.matmul_mx(
-                b_acc[t // 2][:, t % 2, :], lhsT=w2_codes[:, cols].bitcast(FP8X4), lhsT_scale=w2_bytes[:, cols],
+                b_acc[t // 2][:, t % 2, :],
+                lhsT=w2_codes[:, stationary].bitcast(FP8X4), lhsT_scale=w2_bytes[:, stationary],
                 rhs=xo_codes[:].bitcast(FP4X4), rhs_scale=xo_bytes[:], start=True, stop=True,
             )
         for t in range(PACK):
-            b_t = sbuf.tile([P, SLOTS], F32, name="b%d" % t, tag="va%d" % (PACK - 1 - t))
-            nc.scalar.copy(b_t[:], b_acc[t // 2][:, t % 2, :])
-            fetch(bg[:, t, :], b_t, l6[:], sb_t, t)
+            b_plane = sbuf.tile([P, SLOTS], F32, name="b%d" % t, tag="va%d" % (PACK - 1 - t))
+            nc.scalar.copy(b_plane[:], b_acc[t // 2][:, t % 2, :])
+            fetch(b_got[:, t, :], b_plane, b_list[:], sb_t, t)
 
-        pg = sbuf.tile([P, PACK, PLACES], F32, name="pg", tag="va3")
+        pw_got = sbuf.tile([P, PACK, PLACES], F32, name="pw_got", tag="va3")
         for t in range(PACK):
-            fetch(pg[:, t, :], boards[t], l5[:], sa_t, t)
-        hid = sbuf.tile([P, PLACES, PACK], BF16, name="hid", align_bytes=64)
+            fetch(pw_got[:, t, :], boards[t], pw_list[:], sa_t, t)
+        hid = sbuf.tile([P, PLACES, PACK], BF16, name="hid", tag="vc", align_bytes=64)
         hid_codes = sbuf.tile([P, PLACES], U32, name="hid_codes", align_bytes=64)
         hid_bytes = sbuf.tile([P, PLACES], U8, name="hid_bytes", align_bytes=64)
-        halves = [slice(0, PLACES // 2), slice(PLACES // 2, PLACES)]
-        for cols in halves:
+        place_halves = [slice(0, PLACES // 2), slice(PLACES // 2, PLACES)]
+        for cols in place_halves:
             nc.vector.tensor_tensor(
-                hid[:, cols, :].rearrange("p (c i) t -> p c t i", i=4),
-                pg[:, :, cols].rearrange("p t (c i) -> p c t i", i=4),
-                bg[:, :, cols].rearrange("p t (c i) -> p c t i", i=4),
-                MAX,
+                as_words(hid[:, cols, :]), as_planes(pw_got[:, :, cols]), as_planes(b_got[:, :, cols]), MAX
             )
-        for cols in halves:
-            nc.vector.quantize_mx(
-                hid_codes[:, cols].bitcast(FP8X4), hid_bytes[:, cols], hid[:, cols, :].rearrange("p o t -> p (o t)")
-            )
+        for cols in place_halves:
+            quantize(hid_codes, hid_bytes, hid, cols)
 
-        for h in range(OUTS // P):
-            cols = slice(P * h, P * (h + 1))
-            y_acc = psum.tile([P, PLACES], F32, name="y_acc%d" % h)
+        ways_out = ((nc.vector.tensor_copy, nc.sync), (nc.scalar.copy, nc.scalar))
+        for half, (rows, (move, queue)) in enumerate(zip(out_halves, ways_out)):
+            y_acc = psum.tile([P, PLACES], F32, name="y_acc%d" % half)
             nc.tensor.matmul_mx(
-                y_acc[:], lhsT=vc_codes[:, cols].bitcast(FP8X4), lhsT_scale=vc_bytes[:, cols],
+                y_acc[:], lhsT=vc_codes[:, rows].bitcast(FP8X4), lhsT_scale=vc_bytes[:, rows],
                 rhs=hid_codes[:].bitcast(FP8X4), rhs_scale=hid_bytes[:], start=True, stop=True,
             )
-            y = sbuf.tile([P, PLACES], F32, name="y%d" % h)
-            if h == 0:
-                nc.vector.tensor_copy(y[:], y_acc[:])
-                nc.sync.dma_start(out[cols, :], y[:])
-            else:
-                nc.scalar.copy(y[:], y_acc[:])
-                nc.scalar.dma_start(out[cols, :], y[:])
+            y = sbuf.tile([P, PLACES], F32, name="y%d" % half)
+            move(y[:], y_acc[:])
+            queue.dma_start(out[rows, :], y[:])

from contextlib import ExitStack

import concourse.mybir as mybir

F32 = mybir.dt.float32
BF16 = mybir.dt.bfloat16
I32 = mybir.dt.int32
U32 = mybir.dt.uint32
U16 = mybir.dt.uint16
U8 = mybir.dt.uint8
FP8X4 = mybir.dt.float8_e4m3fn_x4
FP4X4 = mybir.dt.float4_e2m1fn_x4
COPY = mybir.ActivationFunctionType.Copy
ADD = mybir.AluOpType.add
MULT = mybir.AluOpType.mult
MAX = mybir.AluOpType.max

P = 128
PACK = 4
QUAD = 32
QUADS = P // QUAD
LIST_ROWS = 16
LINE = 16
SLOTS = 256
PLACES = 128
BOARD = 512
HIDDEN = 512
NOTES = 1024
OUTS = 256
FLOPS = 2 * (2 * 512 * HIDDEN * SLOTS) + 2 * HIDDEN * OUTS * PLACES


def tile_picked_twobooks_plain_two_boardmeet_codes_plain_kernel(
    tc, ta, tb, ga, gb, w_words, w_scales, xo_words, xo_scales, w2_words, w2_scales,
    sa, sb, va, ea, offs, offs2, offs3, offs4, offs5, offs6, offs7, out,
):
    nc = tc.nc
    with ExitStack() as ctx:
        lists = ctx.enter_context(tc.tile_pool(name="lists", bufs=1))
        sbuf = ctx.enter_context(tc.tile_pool(name="sbuf", bufs=1))
        psum = ctx.enter_context(tc.psum_pool(name="psum", bufs=1))

        def load_list(src, name):
            offsets = lists.tile(list(src.shape), U16, name=name)
            nc.sync.dma_start(offsets[:], src)
            return offsets

        def load_factors(src, name):
            factors = sbuf.tile([P, PACK], F32, name=name, tag=name)
            nc.sync.dma_start(factors[:], src.rearrange("(p t) o -> p (t o)", t=PACK))
            return factors

        def load_plane(src, t, name):
            plane = sbuf.tile([P, src.shape[1]], F32, name=name, tag=name)
            nc.sync.dma_start(plane[:], src.rearrange("(p t) c -> p t c", t=PACK)[:, t, :])
            return plane

        def fetch(dst, window, offsets, factors, t):
            nc.scalar.activation(dst, window[:].indirect(offsets), COPY, scale=factors[:, t : t + 1])

        def dealt(columns, run):
            return columns.rearrange("p (t c i) -> p c t i", t=PACK, i=run)

        def undealt(columns, run):
            return columns.rearrange("p (c i t) -> p c t i", t=PACK, i=run)

        def as_words(values):
            return values.rearrange("p (c i) t -> p c t i", i=PACK)

        def as_planes(values):
            return values.rearrange("p t (c i) -> p c t i", i=PACK)

        def quantize(codes, scales, values, cols):
            nc.vector.quantize_mx(
                codes[:, cols].bitcast(FP8X4), scales[:, cols], values[:, cols, :].rearrange("p c t -> p (c t)")
            )

        xo_stage = sbuf.tile([P, 2, NOTES // 4], I32, name="xo_stage")
        nc.vector.memset(xo_stage[P // 2 : P], 0)
        ww_spread = sbuf.tile([P, 2, HIDDEN], U8, name="ww_spread")
        nc.vector.memset(ww_spread[:].rearrange("p s n -> p (s n)").bitcast(I32), 0)
        boards = [sbuf.tile([P, BOARD], F32, name="board%d" % t) for t in range(PACK)]
        for t in range(PACK):
            nc.vector.memset(boards[t][:], 0.0)

        w_raw = sbuf.tile([P, HIDDEN], U16, name="w_raw")
        nc.sync.dma_start(w_raw[:].bitcast(I32), w_words[0].bitcast(I32))
        ta_list = load_list(offs, "ta_list")
        ga_t = load_factors(ga, "ga_t")
        ta_t = [load_plane(ta, 0, "ta0")]
        tb_list = load_list(offs2, "tb_list")
        gb_t = load_factors(gb, "gb_t")
        tb_t = [load_plane(tb, 0, "tb0")]

        ww_stage = sbuf.tile([PACK, QUADS, 2, HIDDEN // 4], I32, name="ww_stage")
        for s, src in enumerate((w_scales, w2_scales)):
            nc.sync.dma_start(ww_stage[:, :, s, :], src[0].bitcast(I32).rearrange("(q i) n -> i q n", i=PACK))
        for q in range(QUADS):
            nc.vector.tensor_copy(
                ww_spread[QUAD * q : QUAD * q + PACK].rearrange("p s n -> p (s n)").bitcast(I32),
                ww_stage[:, q].rearrange("p s n -> p (s n)"),
            )
        ww_bytes = sbuf.tile([P, 2, HIDDEN], U8, name="ww_bytes", align_bytes=64)
        nc.vector.tensor_copy(
            ww_bytes[:].rearrange("p s (t c i) -> p s c t i", t=PACK, i=LINE),
            ww_spread[:].rearrange("p s (c i t) -> p s c t i", t=PACK, i=LINE),
        )
        w_bytes, w2_bytes = ww_bytes[:, 0, :], ww_bytes[:, 1, :]
        ta_t.append(load_plane(ta, 1, "ta1"))

        xo_rows = xo_scales[0].bitcast(I32).rearrange("(u v i) n -> v i u n", u=2, v=2)
        for v in range(2):
            nc.sync.dma_start(xo_stage[P // 2 + QUAD * v : P // 2 + QUAD * v + PACK], xo_rows[v])
        xo_spread = sbuf.tile([P, NOTES], U8, name="xo_spread")
        for u in range(2):
            nc.vector.tensor_copy(
                xo_spread[P // 2 * u : P // 2 * (u + 1), :].bitcast(I32), xo_stage[P // 2 : P, u, :]
            )
        tb_t.append(load_plane(tb, 1, "tb1"))
        xo_list = load_list(offs3, "xo_list")
        for t in range(2, PACK):
            ta_t.append(load_plane(ta, t, "ta%d" % t))
            tb_t.append(load_plane(tb, t, "tb%d" % t))

        va_list = load_list(offs7, "va_list")
        ea_t = load_factors(ea, "ea_t")
        va_t = [load_plane(va, 0, "va0")]
        xo_raw = sbuf.tile([P, NOTES], U16, name="xo_raw", tag="xo_raw")
        nc.sync.dma_start(xo_raw[:].bitcast(I32), xo_words[0].bitcast(I32))
        put_list = load_list(offs4, "put_list")
        va_t.append(load_plane(va, 1, "va1"))
        w2_raw = sbuf.tile([P, HIDDEN], U32, name="w2_raw")
        nc.sync.dma_start(w2_raw[:].bitcast(I32), w2_words[0].rearrange("p n t -> p (n t)").bitcast(I32))
        va_t.append(load_plane(va, 2, "va2"))
        va_t.append(load_plane(va, 3, "va3"))
        b_list = load_list(offs6, "b_list")
        sb_t = load_factors(sb, "sb_t")
        pw_list = load_list(offs5, "pw_list")
        sa_t = load_factors(sa, "sa_t")

        w_codes = sbuf.tile([P, HIDDEN], U16, name="w_codes", align_bytes=64)
        nc.scalar.copy(dealt(w_codes[:], LINE // 2), undealt(w_raw[:], LINE // 2))
        xo_bytes = sbuf.tile([P, SLOTS], U8, name="xo_bytes", align_bytes=64)
        nc.vector.tensor_copy(xo_bytes[:], xo_spread[:].indirect(xo_list[:]))

        xa = sbuf.tile([P, PACK, SLOTS], F32, name="xa")
        xb = sbuf.tile([P, PACK, SLOTS], F32, name="xb", tag="xb", align_bytes=64)
        xc = sbuf.tile([P, SLOTS, PACK], BF16, name="xc", tag="xc", align_bytes=64)
        slot_halves = [slice(0, SLOTS // 2), slice(SLOTS // 2, SLOTS)]

        def entries(offsets, cols):
            return offsets[:, cols.start // LIST_ROWS : cols.stop // LIST_ROWS]

        def add_two_planes(t, cols):
            nc.vector.tensor_tensor(
                xc[:, cols, t : t + 2],
                xa[:, t : t + 2, cols].rearrange("p t j -> p j t"),
                xb[:, t : t + 2, cols].rearrange("p t j -> p j t"),
                ADD,
            )

        for t in range(2):
            fetch(xa[:, t, :], ta_t[t], ta_list[:], ga_t, t)
            fetch(xb[:, t, :], tb_t[t], tb_list[:], gb_t, t)
        add_two_planes(0, slice(0, SLOTS))
        fetch(xa[:, 2, :], ta_t[2], ta_list[:], ga_t, 2)
        fetch(xb[:, 2, :], tb_t[2], tb_list[:], gb_t, 2)
        fetch(xa[:, 3, :], ta_t[3], ta_list[:], ga_t, 3)
        for cols in slot_halves:
            fetch(xb[:, 3, cols], tb_t[3], entries(tb_list, cols), gb_t, 3)
            add_two_planes(2, cols)
        xc_codes = sbuf.tile([P, SLOTS], U32, name="xc_codes", align_bytes=64)
        xc_bytes = sbuf.tile([P, SLOTS], U8, name="xc_bytes", align_bytes=64)
        for cols in slot_halves:
            quantize(xc_codes, xc_bytes, xc, cols)

        w2_codes = sbuf.tile([P, HIDDEN], U32, name="w2_codes", tag="xc", align_bytes=64)
        nc.gpsimd.tensor_copy(dealt(w2_codes[:], LINE // 4), undealt(w2_raw[:], LINE // 4))
        xo_codes = sbuf.tile([P, SLOTS], U16, name="xo_codes", tag="xb", align_bytes=64)
        nc.vector.tensor_copy(xo_codes[:], xo_raw[:].indirect(xo_list[:]))

        a_first = sbuf.tile([P, SLOTS], F32, name="a_first")
        a_rest = sbuf.tile([P, PACK - 1, SLOTS], F32, name="a_rest", tag="xo_raw")
        a_t = [a_first[:]] + [a_rest[:, t, :] for t in range(PACK - 1)]
        pieces = [(0, cols) for cols in slot_halves] + [(t, slice(0, SLOTS)) for t in range(1, PACK)]
        for bank, (t, cols) in enumerate(pieces):
            stationary = slice(P * t, P * (t + 1))
            a_acc = psum.tile([P, cols.stop - cols.start], F32, name="a_acc%d" % bank, tag="bank%d" % bank)
            nc.tensor.matmul_mx(
                a_acc[:], lhsT=w_codes[:, stationary].bitcast(FP4X4), lhsT_scale=w_bytes[:, stationary],
                rhs=xc_codes[:, cols].bitcast(FP8X4), rhs_scale=xc_bytes[:, cols], start=True, stop=True,
            )
            nc.scalar.copy(a_t[t][:, cols], a_acc[:])
        for t, cols in pieces:
            nc.vector.tensor_copy(boards[t][:].indirect(entries(put_list, cols)), a_t[t][:, cols])

        vc_planes = sbuf.tile([P, PACK, OUTS], BF16, name="vc_planes")
        for t in range(PACK):
            fetch(vc_planes[:, t, :], va_t[t], va_list[:], ea_t, t)
        vc_codes = sbuf.tile([P, OUTS], U32, name="vc_codes", align_bytes=64)
        vc_bytes = sbuf.tile([P, OUTS], U8, name="vc_bytes", align_bytes=64)
        vc = sbuf.tile([P, OUTS, PACK], BF16, name="vc", tag="vc", align_bytes=64)
        out_halves = [slice(0, P), slice(P, OUTS)]
        for cols in out_halves:
            nc.gpsimd.tensor_scalar(as_words(vc[:, cols, :]), as_planes(vc_planes[:, :, cols]), 1.0, 0.0, MULT, ADD)
        for cols in out_halves:
            quantize(vc_codes, vc_bytes, vc, cols)

        b_acc = [psum.tile([P, 2, SLOTS], F32, name="b_acc%d" % u, tag="bank%d" % (u + 1)) for u in range(2)]
        b_got = sbuf.tile([P, PACK, PLACES], F32, name="b_got", tag="ea_t")
        for t in range(PACK):
            stationary = slice(P * t, P * (t + 1))
            nc.tensor.matmul_mx(
                b_acc[t // 2][:, t % 2, :],
                lhsT=w2_codes[:, stationary].bitcast(FP8X4), lhsT_scale=w2_bytes[:, stationary],
                rhs=xo_codes[:].bitcast(FP4X4), rhs_scale=xo_bytes[:], start=True, stop=True,
            )
        for t in range(PACK):
            b_plane = sbuf.tile([P, SLOTS], F32, name="b%d" % t, tag="va%d" % (PACK - 1 - t))
            nc.scalar.copy(b_plane[:], b_acc[t // 2][:, t % 2, :])
            fetch(b_got[:, t, :], b_plane, b_list[:], sb_t, t)

        pw_got = sbuf.tile([P, PACK, PLACES], F32, name="pw_got", tag="va3")
        for t in range(PACK):
            fetch(pw_got[:, t, :], boards[t], pw_list[:], sa_t, t)
        hid = sbuf.tile([P, PLACES, PACK], BF16, name="hid", tag="vc", align_bytes=64)
        hid_codes = sbuf.tile([P, PLACES], U32, name="hid_codes", align_bytes=64)
        hid_bytes = sbuf.tile([P, PLACES], U8, name="hid_bytes", align_bytes=64)
        place_halves = [slice(0, PLACES // 2), slice(PLACES // 2, PLACES)]
        for cols in place_halves:
            nc.vector.tensor_tensor(
                as_words(hid[:, cols, :]), as_planes(pw_got[:, :, cols]), as_planes(b_got[:, :, cols]), MAX
            )
        for cols in place_halves:
            quantize(hid_codes, hid_bytes, hid, cols)

        ways_out = ((nc.vector.tensor_copy, nc.sync), (nc.scalar.copy, nc.scalar))
        for half, (rows, (move, queue)) in enumerate(zip(out_halves, ways_out)):
            y_acc = psum.tile([P, PLACES], F32, name="y_acc%d" % half)
            nc.tensor.matmul_mx(
                y_acc[:], lhsT=vc_codes[:, rows].bitcast(FP8X4), lhsT_scale=vc_bytes[:, rows],
                rhs=hid_codes[:].bitcast(FP8X4), rhs_scale=hid_bytes[:], start=True, stop=True,
            )
            y = sbuf.tile([P, PLACES], F32, name="y%d" % half)
            move(y[:], y_acc[:])
            queue.dma_start(out[rows, :], y[:])
